import numpy as np
import ml_dtypes


def mxq(x, axis, fmt="e4m3"):
    dtype, down = {"e4m3": (ml_dtypes.float8_e4m3fn, 7), "e5m2": (ml_dtypes.float8_e5m2, 14)}[fmt]
    v = np.moveaxis(np.asarray(x, np.float32).astype(ml_dtypes.bfloat16).astype(np.float64), axis, -1)
    blocks = v.reshape(v.shape[:-1] + (-1, 32))
    amax = np.abs(blocks).max(-1, keepdims=True)
    byte = np.maximum(np.where(amax > 0, np.frexp(amax)[1] - 1 + 127, 0) - down, 1)
    scale = np.exp2(byte - 127.0)
    codes = (blocks / scale).astype(np.float32).astype(dtype).astype(np.float64)
    return np.moveaxis((codes * scale).reshape(v.shape), -1, axis)


WIDE = False


def mx_kscale(k):
    if not WIDE:
        return np.ones(k)
    levels = np.array([30, -30])
    if k % 512:
        return np.exp2(np.random.permutation(np.resize(levels, k // 32))).repeat(32)
    a = np.empty((k // 512, 16))
    for p in range(k // 512):
        a[p, :8] = np.random.permutation(np.resize(levels, 8))
        for g in range(8):
            far = levels[np.abs(levels - a[p, g]) >= 10]
            a[p, g + 8] = far[np.random.randint(len(far))]
    return np.exp2(a.ravel()).repeat(32)


def f64(x):
    return np.asarray(x).astype(np.float64)


def striped(idx):
    return np.tile(np.asarray(idx).reshape(-1, 16).T, (8, 1)).astype(np.uint16)


def unstriped(offs):
    return offs[:16].T.reshape(-1).astype(np.int64)


K, J, N, T, V, Q = 256, 1024, 256, 2048, 2048, 64


def setup_inputs():
    n = np.random.standard_normal
    idx = np.random.permutation(T)[:J]
    idx2 = np.random.permutation(V)[:J]
    fj = mx_kscale(J)
    return {
        "xf": (n((K, T)) * np.random.uniform(0.4, 1.6, (1, T))).astype(np.float32),
        "ca": (np.random.uniform(0.5, 1.5, (J, 1)) * fj[:, None]).astype(np.float32),
        "gt": (n((N, V)) * np.exp(0.5 * n((1, V)))).astype(np.float32),
        "cb": (np.random.uniform(0.5, 1.5, (J, 1)) / fj[:, None]).astype(np.float32),
        "gk": (np.random.uniform(0.5, 2.0, (K, 1))).astype(np.float32),
        "offs": striped(idx),
        "offs2": striped(idx2),
    }


def reference(xf, ca, gt, cb, gk, offs, offs2):
    idx = unstriped(offs)
    idx2 = unstriped(offs2)
    xj = f64(xf)[:, idx].T
    uj = xj / (np.mean(np.abs(xj), axis=1, keepdims=True) + 0.1) * f64(ca)
    gr1 = f64(gt)[:, idx2].T
    gj = gr1 / (np.max(np.abs(gr1), axis=1, keepdims=True) + 0.2) * f64(cb)
    ujq = mxq(uj, 0, "e4m3")
    gjq = mxq(gj, 0, "e5m2")
    w = ujq.T @ gjq
    wq = w.reshape(K, Q, N // Q).sum(axis=2)
    y = 0.02 * wq * f64(gk)
    return y

@@ -1,0 +1,187 @@
+from contextlib import ExitStack
+
+import concourse.mybir as mybir
+from concourse.masks import make_identity
+
+K, J, N, T, Q = 256, 1024, 256, 2048, 64
+FLOPS = 2 * K * J * N
+
+F32 = mybir.dt.float32
+BF16 = mybir.dt.bfloat16
+U32 = mybir.dt.uint32
+U16 = mybir.dt.uint16
+U8 = mybir.dt.uint8
+E4M3 = mybir.dt.float8_e4m3fn_x4
+E5M2 = mybir.dt.float8_e5m2_x4
+ALU = mybir.AluOpType
+ACT = mybir.ActivationFunctionType
+AXIS_X = mybir.AxisListType.X
+
+P = 128
+PACK = 4
+SLOTS = P * PACK
+PASSES = J // SLOTS
+HALVES = 2
+LIST_COLS = SLOTS // 16
+
+
+def tile_list_moment_sized_sized_sums_kernel(tc, xf, ca, gt, cb, gk, offs, offs2, out):
+    nc = tc.nc
+    with ExitStack() as ctx:
+        sb = ctx.enter_context(tc.tile_pool(name="sb", bufs=1))
+        ps = ctx.enter_context(tc.psum_pool(name="ps", bufs=1))
+
+        g_list = sb.tile([P, J // 16], U16, name="g_list")
+        x_list = sb.tile([P, J // 16], U16, name="x_list")
+        g_rows = [sb.tile([P, T], F32, name="g_rows%d" % h) for h in range(HALVES)]
+        x_rows = [sb.tile([P, T], F32, name="x_rows%d" % h) for h in range(HALVES)]
+        g_weight = sb.tile([P, PASSES, PACK], F32, name="g_weight")
+        x_weight = sb.tile([P, PASSES, PACK], F32, name="x_weight")
+        row_factor = sb.tile([P, HALVES], F32, name="row_factor")
+        out_factor = sb.tile([P, HALVES], F32, name="out_factor")
+        identity = sb.tile([P, P], F32, name="identity")
+
+        gt_halves = gt.rearrange("(p h) v -> h p v", h=HALVES)
+        xf_halves = xf.rearrange("(p h) v -> h p v", h=HALVES)
+        nc.sync.dma_start(g_list[:], offs2)
+        for h in range(HALVES):
+            nc.sync.dma_start(g_rows[h][:], gt_halves[h])
+        nc.sync.dma_start(x_list[:], offs)
+        for h in range(HALVES):
+            nc.sync.dma_start(x_rows[h][:], xf_halves[h])
+        nc.scalar.dma_start(row_factor[:], gk.rearrange("(p h) o -> p (h o)", h=HALVES))
+        nc.scalar.dma_start(g_weight[:], cb.rearrange("(a p t) o -> p a (t o)", a=PASSES, t=PACK))
+        nc.scalar.dma_start(x_weight[:], ca.rearrange("(a p t) o -> p a (t o)", a=PASSES, t=PACK))
+        make_identity(nc, identity[:])
+        nc.scalar.activation(out_factor[:], row_factor[:], ACT.Copy, scale=0.02)
+
+        banks = {}
+
+        def gather_and_turn(side, rows, slot_list, h, a, on_vector):
+            picked = sb.tile([P, SLOTS], F32, name="picked_%s%d%d" % (side, h, a))
+            offsets = slot_list[:, a * LIST_COLS : (a + 1) * LIST_COLS]
+            if on_vector:
+                nc.vector.tensor_copy(
+                    picked[:].bitcast(U32).rearrange("p (t s) -> p s t", t=PACK),
+                    rows[h][:].bitcast(U32).indirect(offsets),
+                )
+                planes = picked[:].rearrange("p (t s) -> p t s", t=PACK)
+            else:
+                nc.scalar.activation(picked[:], rows[h][:].indirect(offsets), ACT.Copy)
+                planes = picked[:].rearrange("p (s t) -> p t s", t=PACK)
+            bank = ps.tile([P, PACK, P], F32, name="turned_%s%d%d" % (side, h, a), tag="bank_%s%d%d" % (side, h, a))
+            for t in range(PACK):
+                nc.tensor.transpose(bank[:, t, :], planes[:, t, :], identity[:])
+            banks[side, h, a] = bank
+
+        g_top = {}
+
+        def g_stat(h, a):
+            magnitude = sb.tile([P, PACK, P], F32, name="magnitude%d%d" % (h, a))
+            nc.scalar.activation(magnitude[:], banks["g", h, a][:], ACT.Abs)
+            top = sb.tile([P, PACK], F32, name="g_top%d%d" % (h, a))
+            nc.vector.tensor_reduce(top[:], magnitude[:], AXIS_X, ALU.max)
+            g_top[h, a] = top
+
+        x_mean = {}
+
+        def x_stat(h, a):
+            unused = sb.tile([P, PACK, P], BF16, name="x_magnitude%d%d" % (h, a))
+            part = sb.tile([P, PACK], F32, name="x_mean%d%d" % (h, a))
+            for t in range(PACK):
+                nc.scalar.activation(
+                    unused[:, t, :], banks["x", h, a][:, t, :], ACT.Abs, scale=1.0 / K, accum_out=part[:, t : t + 1]
+                )
+            x_mean[h, a] = part
+
+        factors = {}
+
+        def finish_factor(side, a, size, weight):
+            inverse = sb.tile([P, PACK], F32, name="inverse_%s%d" % (side, a))
+            nc.vector.reciprocal(inverse[:], size[:])
+            factor = sb.tile([P, PACK], F32, name="factor_%s%d" % (side, a))
+            nc.vector.tensor_tensor(factor[:], inverse[:], weight[:, a, :], ALU.mult)
+            factors[side, a] = factor
+
+        def g_factor(a):
+            shifted = sb.tile([P, PACK], F32, name="g_shifted%d" % a)
+            nc.vector.tensor_scalar(shifted[:], g_top[0, a][:], 0.2, None, ALU.add)
+            size = sb.tile([P, PACK], F32, name="g_size%d" % a)
+            nc.vector.scalar_tensor_tensor(size[:], g_top[1, a][:], 0.2, shifted[:], ALU.add, ALU.max)
+            finish_factor("g", a, size, g_weight)
+
+        def x_factor(a):
+            size = sb.tile([P, PACK], F32, name="x_size%d" % a)
+            nc.vector.scalar_tensor_tensor(size[:], x_mean[1, a][:], 0.1, x_mean[0, a][:], ALU.add, ALU.add)
+            finish_factor("x", a, size, x_weight)
+
+        rounded = {}
+
+        def scale(side, h, a):
+            tile = sb.tile([P, P, PACK], BF16, name="rounded_%s%d%d" % (side, h, a), align_bytes=64)
+            nc.vector.tensor_tensor(
+                tile[:],
+                banks[side, h, a][:].rearrange("p t c -> p c t"),
+                factors[side, a][:].unsqueeze(1).to_broadcast([P, P, PACK]),
+                ALU.mult,
+            )
+            rounded[side, h, a] = tile
+
+        operand = {}
+
+        def quantize(side, h, a, fmt):
+            codes = sb.tile([P, P], U32, name="codes_%s%d%d" % (side, h, a), align_bytes=64)
+            scales = sb.tile([P, P], U8, name="scales_%s%d%d" % (side, h, a), align_bytes=64)
+            nc.vector.quantize_mx(
+                out=codes[:].bitcast(fmt), scales=scales[:], in_=rounded[side, h, a][:].rearrange("p c t -> p (c t)")
+            )
+            operand[side, h, a] = (codes[:].bitcast(fmt), scales[:])
+
+        for h in range(HALVES):
+            gather_and_turn("g", g_rows, g_list, h, 0, True)
+            gather_and_turn("g", g_rows, g_list, h, 1, False)
+        for h in range(HALVES):
+            for a in range(PASSES):
+                g_stat(h, a)
+        gather_and_turn("x", x_rows, x_list, 0, 0, False)
+        gather_and_turn("x", x_rows, x_list, 1, 0, True)
+        gather_and_turn("x", x_rows, x_list, 0, 1, False)
+        gather_and_turn("x", x_rows, x_list, 1, 1, False)
+        for a in range(PASSES):
+            g_factor(a)
+        for a in range(PASSES):
+            for h in range(HALVES):
+                x_stat(h, a)
+        for a in range(PASSES):
+            for h in range(HALVES):
+                scale("g", h, a)
+        for a in range(PASSES):
+            x_factor(a)
+        for a in range(PASSES):
+            for h in range(HALVES):
+                quantize("g", h, a, E5M2)
+        for a in range(PASSES):
+            for h in range(HALVES):
+                scale("x", h, a)
+            for h in range(HALVES):
+                quantize("x", h, a, E4M3)
+
+        out_halves = out.rearrange("(p h) q -> h p q", h=HALVES)
+        for m in range(HALVES):
+            pair_sums = ps.tile([P, Q, 2], F32, name="pair_sums%d" % m, tag="bank_g%d0" % m)
+            for a in range(PASSES):
+                for h in range(HALVES):
+                    nc.tensor.matmul_mx(
+                        out=pair_sums[:].rearrange("p q e -> p (q e)"),
+                        lhsT=operand["x", m, a][0],
+                        lhsT_scale=operand["x", m, a][1],
+                        rhs=operand["g", h, a][0],
+                        rhs_scale=operand["g", h, a][1],
+                        start=(a == 0 and h == 0),
+                        stop=(a == PASSES - 1 and h == HALVES - 1),
+                    )
+            set_sums = sb.tile([P, Q], F32, name="set_sums%d" % m)
+            nc.vector.tensor_reduce(set_sums[:], pair_sums[:], AXIS_X, ALU.add)
+            result = sb.tile([P, Q], F32, name="result%d" % m)
+            nc.vector.tensor_scalar(result[:], set_sums[:], out_factor[:, m : m + 1], None, ALU.mult)
+            nc.sync.dma_start(out_halves[m], result[:])

@@ -35,8 +35,8 @@ def tile_list_moment_sized_sized_sums_kernel(tc, xf, ca, gt, cb, gk, offs, offs2
         x_list = sb.tile([P, J // 16], U16, name="x_list")
         g_rows = [sb.tile([P, T], F32, name="g_rows%d" % h) for h in range(HALVES)]
         x_rows = [sb.tile([P, T], F32, name="x_rows%d" % h) for h in range(HALVES)]
-        g_weight = sb.tile([P, PASSES, PACK], F32, name="g_weight")
-        x_weight = sb.tile([P, PASSES, PACK], F32, name="x_weight")
+        g_pairs = sb.tile([P, PASSES, 2, PACK], F32, name="g_pairs")
+        x_pairs = sb.tile([P, PASSES, 2, PACK], F32, name="x_pairs")
         row_factor = sb.tile([P, HALVES], F32, name="row_factor")
         out_factor = sb.tile([P, HALVES], F32, name="out_factor")
         identity = sb.tile([P, P], F32, name="identity")
@@ -50,15 +50,15 @@ def tile_list_moment_sized_sized_sums_kernel(tc, xf, ca, gt, cb, gk, offs, offs2
         for h in range(HALVES):
             nc.sync.dma_start(x_rows[h][:], xf_halves[h])
         nc.scalar.dma_start(row_factor[:], gk.rearrange("(p h) o -> p (h o)", h=HALVES))
-        nc.scalar.dma_start(g_weight[:], cb.rearrange("(a p t) o -> p a (t o)", a=PASSES, t=PACK))
-        nc.scalar.dma_start(x_weight[:], ca.rearrange("(a p t) o -> p a (t o)", a=PASSES, t=PACK))
+        nc.scalar.dma_start(g_pairs[:, :, 1, :], cb.rearrange("(a p t) o -> p a (t o)", a=PASSES, t=PACK))
+        nc.scalar.dma_start(x_pairs[:, :, 1, :], ca.rearrange("(a p t) o -> p a (t o)", a=PASSES, t=PACK))
         make_identity(nc, identity[:])
         nc.scalar.activation(out_factor[:], row_factor[:], ACT.Copy, scale=0.02)
 
         banks = {}
 
-        def gather_and_turn(side, rows, slot_list, h, a, on_vector):
-            picked = sb.tile([P, SLOTS], F32, name="picked_%s%d%d" % (side, h, a))
+        def gather_and_turn(side, rows, slot_list, h, a, on_vector, buffer):
+            picked = sb.tile([P, SLOTS], F32, name="picked_%s%d%d" % (side, h, a), tag=buffer)
             offsets = slot_list[:, a * LIST_COLS : (a + 1) * LIST_COLS]
             if on_vector:
                 nc.vector.tensor_copy(
@@ -74,97 +74,124 @@ def tile_list_moment_sized_sized_sums_kernel(tc, xf, ca, gt, cb, gk, offs, offs2
                 nc.tensor.transpose(bank[:, t, :], planes[:, t, :], identity[:])
             banks[side, h, a] = bank
 
-        g_top = {}
+        x_terms = sb.tile([P, PASSES, HALVES + 1, PACK], F32, name="x_terms")
+        nc.vector.tensor_scalar(
+            x_terms[:, :, HALVES, :],
+            identity[:, 0 : PASSES * PACK].rearrange("p (a t) -> p a t", t=PACK),
+            0.0,
+            0.1,
+            ALU.mult,
+            ALU.add,
+        )
+
+        g_turned = {}
+        g_top = sb.tile([P, HALVES, PASSES, PACK], F32, name="g_top")
 
         def g_stat(h, a):
-            magnitude = sb.tile([P, PACK, P], F32, name="magnitude%d%d" % (h, a))
-            nc.scalar.activation(magnitude[:], banks["g", h, a][:], ACT.Abs)
-            top = sb.tile([P, PACK], F32, name="g_top%d%d" % (h, a))
-            nc.vector.tensor_reduce(top[:], magnitude[:], AXIS_X, ALU.max)
-            g_top[h, a] = top
-
-        x_mean = {}
+            tile = sb.tile([P, PACK, P], F32, name="g_turned%d%d" % (h, a), tag="g_turned%d%d" % (h, a))
+            nc.scalar.copy(tile[:], banks["g", h, a][:])
+            nc.vector.tensor_reduce(g_top[:, h, a, :], tile[:], AXIS_X, ALU.max, apply_absolute_value=True)
+            g_turned[h, a] = tile
 
         def x_stat(h, a):
             unused = sb.tile([P, PACK, P], BF16, name="x_magnitude%d%d" % (h, a))
-            part = sb.tile([P, PACK], F32, name="x_mean%d%d" % (h, a))
             for t in range(PACK):
                 nc.scalar.activation(
-                    unused[:, t, :], banks["x", h, a][:, t, :], ACT.Abs, scale=1.0 / K, accum_out=part[:, t : t + 1]
+                    unused[:, t, :],
+                    banks["x", h, a][:, t, :],
+                    ACT.Abs,
+                    scale=1.0 / K,
+                    accum_out=x_terms[:, a, h, t : t + 1],
                 )
-            x_mean[h, a] = part
 
         factors = {}
 
-        def finish_factor(side, a, size, weight):
-            inverse = sb.tile([P, PACK], F32, name="inverse_%s%d" % (side, a))
-            nc.vector.reciprocal(inverse[:], size[:])
-            factor = sb.tile([P, PACK], F32, name="factor_%s%d" % (side, a))
-            nc.vector.tensor_tensor(factor[:], inverse[:], weight[:, a, :], ALU.mult)
-            factors[side, a] = factor
-
         def g_factor(a):
-            shifted = sb.tile([P, PACK], F32, name="g_shifted%d" % a)
-            nc.vector.tensor_scalar(shifted[:], g_top[0, a][:], 0.2, None, ALU.add)
+            shifted = sb.tile([P, PACK], F32, name="g_shifted%d" % a, tag="g_shifted%d" % a)
+            nc.vector.tensor_scalar(shifted[:], g_top[:, 0, a], 0.2, None, ALU.add)
             size = sb.tile([P, PACK], F32, name="g_size%d" % a)
-            nc.vector.scalar_tensor_tensor(size[:], g_top[1, a][:], 0.2, shifted[:], ALU.add, ALU.max)
-            finish_factor("g", a, size, g_weight)
+            nc.vector.scalar_tensor_tensor(size[:], g_top[:, 1, a], 0.2, shifted[:], ALU.add, ALU.max)
+            pair = g_pairs[:, a]
+            nc.vector.reciprocal(pair[:, 0, :], size[:])
+            factor = sb.tile([P, PACK], F32, name="g_factor%d" % a)
+            nc.vector.tensor_reduce(factor[:], pair.rearrange("p i t -> p t i"), AXIS_X, ALU.mult)
+            factors["g", a] = factor[:].unsqueeze(1).to_broadcast([P, P, PACK])
 
         def x_factor(a):
             size = sb.tile([P, PACK], F32, name="x_size%d" % a)
-            nc.vector.scalar_tensor_tensor(size[:], x_mean[1, a][:], 0.1, x_mean[0, a][:], ALU.add, ALU.add)
-            finish_factor("x", a, size, x_weight)
+            nc.vector.tensor_reduce(size[:], x_terms[:, a].rearrange("p i t -> p t i"), AXIS_X, ALU.add)
+            pair = x_pairs[:, a]
+            nc.vector.reciprocal(pair[:, 0, :], size[:])
+            factor = sb.tile([P, PACK], F32, name="x_factor%d" % a, tag="x_factor%d" % a, align_bytes=64)
+            nc.vector.tensor_reduce(factor[:], pair.rearrange("p i t -> p t i"), AXIS_X, ALU.mult)
+            factors["x", a] = factor[:].unsqueeze(1).to_broadcast([P, P, PACK])
 
-        rounded = {}
+        g_rounded = sb.tile([P, PASSES, HALVES, P, PACK], BF16, name="g_rounded", align_bytes=64)
+        x_rounded = {}
 
-        def scale(side, h, a):
-            tile = sb.tile([P, P, PACK], BF16, name="rounded_%s%d%d" % (side, h, a), align_bytes=64)
-            nc.vector.tensor_tensor(
-                tile[:],
-                banks[side, h, a][:].rearrange("p t c -> p c t"),
-                factors[side, a][:].unsqueeze(1).to_broadcast([P, P, PACK]),
-                ALU.mult,
-            )
-            rounded[side, h, a] = tile
+        def g_scale(h, a):
+            if h == a:
+                engine, source = nc.vector, banks["g", h, a]
+            else:
+                engine, source = nc.gpsimd, g_turned[h, a]
+            engine.tensor_tensor(g_rounded[:, a, h], source[:].rearrange("p t c -> p c t"), factors["g", a], ALU.mult)
+
+        def x_scale(h, a):
+            tile = sb.tile([P, P, PACK], BF16, name="x_rounded%d%d" % (h, a), align_bytes=64)
+            nc.vector.tensor_tensor(tile[:], banks["x", h, a][:].rearrange("p t c -> p c t"), factors["x", a], ALU.mult)
+            x_rounded[h, a] = tile
 
         operand = {}
 
-        def quantize(side, h, a, fmt):
-            codes = sb.tile([P, P], U32, name="codes_%s%d%d" % (side, h, a), align_bytes=64)
-            scales = sb.tile([P, P], U8, name="scales_%s%d%d" % (side, h, a), align_bytes=64)
+        def g_quantize():
+            codes = sb.tile([P, PASSES * HALVES * P], U32, name="g_codes", tag="x_factor0", align_bytes=64)
+            scales = sb.tile([P, PASSES * HALVES * P], U8, name="g_scales", align_bytes=64)
             nc.vector.quantize_mx(
-                out=codes[:].bitcast(fmt), scales=scales[:], in_=rounded[side, h, a][:].rearrange("p c t -> p (c t)")
+                out=codes[:].bitcast(E5M2), scales=scales[:], in_=g_rounded[:].rearrange("p a h c t -> p (a h c t)")
             )
-            operand[side, h, a] = (codes[:].bitcast(fmt), scales[:])
-
-        for h in range(HALVES):
-            gather_and_turn("g", g_rows, g_list, h, 0, True)
-            gather_and_turn("g", g_rows, g_list, h, 1, False)
-        for h in range(HALVES):
             for a in range(PASSES):
-                g_stat(h, a)
-        gather_and_turn("x", x_rows, x_list, 0, 0, False)
-        gather_and_turn("x", x_rows, x_list, 1, 0, True)
-        gather_and_turn("x", x_rows, x_list, 0, 1, False)
-        gather_and_turn("x", x_rows, x_list, 1, 1, False)
-        for a in range(PASSES):
-            g_factor(a)
+                for h in range(HALVES):
+                    cols = slice((a * HALVES + h) * P, (a * HALVES + h + 1) * P)
+                    operand["g", h, a] = (codes[:, cols].bitcast(E5M2), scales[:, cols])
+
+        def x_quantize(h, a):
+            codes = sb.tile([P, P], U32, name="x_codes%d%d" % (h, a), align_bytes=64)
+            scales = sb.tile([P, P], U8, name="x_scales%d%d" % (h, a), align_bytes=64)
+            nc.vector.quantize_mx(
+                out=codes[:].bitcast(E4M3), scales=scales[:], in_=x_rounded[h, a][:].rearrange("p c t -> p (c t)")
+            )
+            operand["x", h, a] = (codes[:].bitcast(E4M3), scales[:])
+
+        gather_and_turn("g", g_rows, g_list, 0, 0, True, "picked_a")
+        gather_and_turn("g", g_rows, g_list, 0, 1, False, "picked_b")
+        g_stat(0, 0)
+        gather_and_turn("g", g_rows, g_list, 1, 0, True, "picked_c")
+        gather_and_turn("g", g_rows, g_list, 1, 1, False, "picked_a")
+        g_stat(0, 1)
+        g_stat(1, 0)
+        g_factor(0)
+        gather_and_turn("x", x_rows, x_list, 0, 0, True, "g_turned00")
+        gather_and_turn("x", x_rows, x_list, 0, 1, False, "picked_c")
+        gather_and_turn("x", x_rows, x_list, 1, 0, True, "g_shifted0")
+        g_stat(1, 1)
+        g_factor(1)
+        gather_and_turn("x", x_rows, x_list, 1, 1, False, "picked_a")
         for a in range(PASSES):
             for h in range(HALVES):
                 x_stat(h, a)
-        for a in range(PASSES):
-            for h in range(HALVES):
-                scale("g", h, a)
-        for a in range(PASSES):
-            x_factor(a)
-        for a in range(PASSES):
-            for h in range(HALVES):
-                quantize("g", h, a, E5M2)
-        for a in range(PASSES):
-            for h in range(HALVES):
-                scale("x", h, a)
-            for h in range(HALVES):
-                quantize("x", h, a, E4M3)
+        for h, a in ((1, 0), (0, 0), (0, 1), (1, 1)):
+            g_scale(h, a)
+        x_factor(0)
+        for h in range(HALVES):
+            x_scale(h, 0)
+        x_factor(1)
+        g_quantize()
+        for h in range(HALVES):
+            x_quantize(h, 0)
+        for h in range(HALVES):
+            x_scale(h, 1)
+        for h in range(HALVES):
+            x_quantize(h, 1)
 
         out_halves = out.rearrange("(p h) q -> h p q", h=HALVES)
         for m in range(HALVES):

@@ -23,6 +23,8 @@ SLOTS = P * PACK
 PASSES = J // SLOTS
 HALVES = 2
 LIST_COLS = SLOTS // 16
+RUN = 8
+WEIGHT_ROW = {"g": 0, "x": PACK}
 
 
 def tile_list_moment_sized_sized_sums_kernel(tc, xf, ca, gt, cb, gk, offs, offs2, out):
@@ -35,25 +37,29 @@ def tile_list_moment_sized_sized_sums_kernel(tc, xf, ca, gt, cb, gk, offs, offs2
         x_list = sb.tile([P, J // 16], U16, name="x_list")
         g_rows = [sb.tile([P, T], F32, name="g_rows%d" % h) for h in range(HALVES)]
         x_rows = [sb.tile([P, T], F32, name="x_rows%d" % h) for h in range(HALVES)]
-        g_pairs = sb.tile([P, PASSES, 2, PACK], F32, name="g_pairs")
-        x_pairs = sb.tile([P, PASSES, 2, PACK], F32, name="x_pairs")
+        pairs = {side: sb.tile([P, 2, PACK], F32, name="pairs_" + side) for side in "gx"}
+        weight_rows = sb.tile([P, P], F32, name="weight_rows")
         row_factor = sb.tile([P, HALVES], F32, name="row_factor")
-        out_factor = sb.tile([P, HALVES], F32, name="out_factor")
         identity = sb.tile([P, P], F32, name="identity")
 
         gt_halves = gt.rearrange("(p h) v -> h p v", h=HALVES)
         xf_halves = xf.rearrange("(p h) v -> h p v", h=HALVES)
+        nc.vector.memset(weight_rows[:], 0.0)
+        make_identity(nc, identity[:])
         nc.sync.dma_start(g_list[:], offs2)
         for h in range(HALVES):
             nc.sync.dma_start(g_rows[h][:], gt_halves[h])
         nc.sync.dma_start(x_list[:], offs)
         for h in range(HALVES):
             nc.sync.dma_start(x_rows[h][:], xf_halves[h])
-        nc.scalar.dma_start(row_factor[:], gk.rearrange("(p h) o -> p (h o)", h=HALVES))
-        nc.scalar.dma_start(g_pairs[:, :, 1, :], cb.rearrange("(a p t) o -> p a (t o)", a=PASSES, t=PACK))
-        nc.scalar.dma_start(x_pairs[:, :, 1, :], ca.rearrange("(a p t) o -> p a (t o)", a=PASSES, t=PACK))
-        make_identity(nc, identity[:])
-        nc.scalar.activation(out_factor[:], row_factor[:], ACT.Copy, scale=0.02)
+        for side, weight in (("g", cb), ("x", ca)):
+            first = WEIGHT_ROW[side]
+            nc.scalar.dma_start(
+                weight_rows[first : first + PACK, :].rearrange("t (b r) -> t b r", r=RUN),
+                weight[0:SLOTS].rearrange("(b t r) o -> t b (r o)", t=PACK, r=RUN),
+            )
+            nc.sync.dma_start(pairs[side][:, 1, :], weight[SLOTS:J].rearrange("(p t) o -> p (t o)", t=PACK))
+        nc.sync.dma_start(row_factor[:], gk.rearrange("(p h) o -> p (h o)", h=HALVES))
 
         banks = {}
 
@@ -62,7 +68,7 @@ def tile_list_moment_sized_sized_sums_kernel(tc, xf, ca, gt, cb, gk, offs, offs2
             offsets = slot_list[:, a * LIST_COLS : (a + 1) * LIST_COLS]
             if on_vector:
                 nc.vector.tensor_copy(
-                    picked[:].bitcast(U32).rearrange("p (t s) -> p s t", t=PACK),
+                    picked[:].bitcast(U32).rearrange("p (t b r) -> p b t r", t=PACK, r=RUN),
                     rows[h][:].bitcast(U32).indirect(offsets),
                 )
                 planes = picked[:].rearrange("p (t s) -> p t s", t=PACK)
@@ -75,14 +81,9 @@ def tile_list_moment_sized_sized_sums_kernel(tc, xf, ca, gt, cb, gk, offs, offs2
             banks[side, h, a] = bank
 
         x_terms = sb.tile([P, PASSES, HALVES + 1, PACK], F32, name="x_terms")
-        nc.vector.tensor_scalar(
-            x_terms[:, :, HALVES, :],
-            identity[:, 0 : PASSES * PACK].rearrange("p (a t) -> p a t", t=PACK),
-            0.0,
-            0.1,
-            ALU.mult,
-            ALU.add,
-        )
+        zeros = sb.tile([P, PASSES, PACK], F32, name="zeros")
+        nc.vector.memset(zeros[:], 0.0)
+        nc.scalar.activation(x_terms[:, :, HALVES, :], zeros[:], ACT.Copy, bias=0.1)
 
         g_turned = {}
         g_top = sb.tile([P, HALVES, PASSES, PACK], F32, name="g_top")
@@ -106,25 +107,36 @@ def tile_list_moment_sized_sized_sums_kernel(tc, xf, ca, gt, cb, gk, offs, offs2
 
         factors = {}
 
+        turned_weights = []
+
+        def turn_weights():
+            bank = ps.tile([P, P], F32, name="turned_weights", tag="bank_g01")
+            nc.tensor.transpose(bank[:], weight_rows[:], identity[:])
+            turned_weights.append(bank)
+
+        def finish_factor(side, a, size):
+            factor = sb.tile([P, PACK], F32, name="factor_%s%d" % (side, a), tag="factor_%s%d" % (side, a), align_bytes=64)
+            if a == 0:
+                inverse = sb.tile([P, PACK], F32, name="inverse_" + side)
+                nc.vector.reciprocal(inverse[:], size[:])
+                weight = turned_weights[0][:, WEIGHT_ROW[side] : WEIGHT_ROW[side] + PACK]
+                nc.vector.tensor_tensor(factor[:], inverse[:], weight, ALU.mult)
+            else:
+                nc.vector.reciprocal(pairs[side][:, 0, :], size[:])
+                nc.vector.tensor_reduce(factor[:], pairs[side][:].rearrange("p i t -> p t i"), AXIS_X, ALU.mult)
+            factors[side, a] = factor[:].unsqueeze(1).to_broadcast([P, P, PACK])
+
         def g_factor(a):
             shifted = sb.tile([P, PACK], F32, name="g_shifted%d" % a, tag="g_shifted%d" % a)
             nc.vector.tensor_scalar(shifted[:], g_top[:, 0, a], 0.2, None, ALU.add)
             size = sb.tile([P, PACK], F32, name="g_size%d" % a)
             nc.vector.scalar_tensor_tensor(size[:], g_top[:, 1, a], 0.2, shifted[:], ALU.add, ALU.max)
-            pair = g_pairs[:, a]
-            nc.vector.reciprocal(pair[:, 0, :], size[:])
-            factor = sb.tile([P, PACK], F32, name="g_factor%d" % a)
-            nc.vector.tensor_reduce(factor[:], pair.rearrange("p i t -> p t i"), AXIS_X, ALU.mult)
-            factors["g", a] = factor[:].unsqueeze(1).to_broadcast([P, P, PACK])
+            finish_factor("g", a, size)
 
         def x_factor(a):
             size = sb.tile([P, PACK], F32, name="x_size%d" % a)
             nc.vector.tensor_reduce(size[:], x_terms[:, a].rearrange("p i t -> p t i"), AXIS_X, ALU.add)
-            pair = x_pairs[:, a]
-            nc.vector.reciprocal(pair[:, 0, :], size[:])
-            factor = sb.tile([P, PACK], F32, name="x_factor%d" % a, tag="x_factor%d" % a, align_bytes=64)
-            nc.vector.tensor_reduce(factor[:], pair.rearrange("p i t -> p t i"), AXIS_X, ALU.mult)
-            factors["x", a] = factor[:].unsqueeze(1).to_broadcast([P, P, PACK])
+            finish_factor("x", a, size)
 
         g_rounded = sb.tile([P, PASSES, HALVES, P, PACK], BF16, name="g_rounded", align_bytes=64)
         x_rounded = {}
@@ -144,7 +156,7 @@ def tile_list_moment_sized_sized_sums_kernel(tc, xf, ca, gt, cb, gk, offs, offs2
         operand = {}
 
         def g_quantize():
-            codes = sb.tile([P, PASSES * HALVES * P], U32, name="g_codes", tag="x_factor0", align_bytes=64)
+            codes = sb.tile([P, PASSES * HALVES * P], U32, name="g_codes", tag="factor_x0", align_bytes=64)
             scales = sb.tile([P, PASSES * HALVES * P], U8, name="g_scales", align_bytes=64)
             nc.vector.quantize_mx(
                 out=codes[:].bitcast(E5M2), scales=scales[:], in_=g_rounded[:].rearrange("p a h c t -> p (a h c t)")
@@ -168,6 +180,7 @@ def tile_list_moment_sized_sized_sums_kernel(tc, xf, ca, gt, cb, gk, offs, offs2
         gather_and_turn("g", g_rows, g_list, 1, 0, True, "picked_c")
         gather_and_turn("g", g_rows, g_list, 1, 1, False, "picked_a")
         g_stat(0, 1)
+        turn_weights()
         g_stat(1, 0)
         g_factor(0)
         gather_and_turn("x", x_rows, x_list, 0, 0, True, "g_turned00")
@@ -195,7 +208,7 @@ def tile_list_moment_sized_sized_sums_kernel(tc, xf, ca, gt, cb, gk, offs, offs2
 
         out_halves = out.rearrange("(p h) q -> h p q", h=HALVES)
         for m in range(HALVES):
-            pair_sums = ps.tile([P, Q, 2], F32, name="pair_sums%d" % m, tag="bank_g%d0" % m)
+            pair_sums = ps.tile([P, Q, 2], F32, name="pair_sums%d" % m, tag="bank_g%d%d" % (m, m))
             for a in range(PASSES):
                 for h in range(HALVES):
                     nc.tensor.matmul_mx(
@@ -210,5 +223,5 @@ def tile_list_moment_sized_sized_sums_kernel(tc, xf, ca, gt, cb, gk, offs, offs2
             set_sums = sb.tile([P, Q], F32, name="set_sums%d" % m)
             nc.vector.tensor_reduce(set_sums[:], pair_sums[:], AXIS_X, ALU.add)
             result = sb.tile([P, Q], F32, name="result%d" % m)
-            nc.vector.tensor_scalar(result[:], set_sums[:], out_factor[:, m : m + 1], None, ALU.mult)
+            nc.vector.tensor_scalar(result[:], set_sums[:], row_factor[:, m : m + 1], 0.02, ALU.mult, ALU.mult)
             nc.sync.dma_start(out_halves[m], result[:])

@@ -23,8 +23,6 @@ SLOTS = P * PACK
 PASSES = J // SLOTS
 HALVES = 2
 LIST_COLS = SLOTS // 16
-RUN = 8
-WEIGHT_ROW = {"g": 0, "x": PACK}
 
 
 def tile_list_moment_sized_sized_sums_kernel(tc, xf, ca, gt, cb, gk, offs, offs2, out):
@@ -37,29 +35,25 @@ def tile_list_moment_sized_sized_sums_kernel(tc, xf, ca, gt, cb, gk, offs, offs2
         x_list = sb.tile([P, J // 16], U16, name="x_list")
         g_rows = [sb.tile([P, T], F32, name="g_rows%d" % h) for h in range(HALVES)]
         x_rows = [sb.tile([P, T], F32, name="x_rows%d" % h) for h in range(HALVES)]
-        pairs = {side: sb.tile([P, 2, PACK], F32, name="pairs_" + side) for side in "gx"}
-        weight_rows = sb.tile([P, P], F32, name="weight_rows")
+        g_pairs = sb.tile([P, PASSES, 2, PACK], F32, name="g_pairs")
+        x_pairs = sb.tile([P, PASSES, 2, PACK], F32, name="x_pairs")
         row_factor = sb.tile([P, HALVES], F32, name="row_factor")
+        out_factor = sb.tile([P, HALVES], F32, name="out_factor")
         identity = sb.tile([P, P], F32, name="identity")
 
         gt_halves = gt.rearrange("(p h) v -> h p v", h=HALVES)
         xf_halves = xf.rearrange("(p h) v -> h p v", h=HALVES)
-        nc.vector.memset(weight_rows[:], 0.0)
-        make_identity(nc, identity[:])
         nc.sync.dma_start(g_list[:], offs2)
         for h in range(HALVES):
             nc.sync.dma_start(g_rows[h][:], gt_halves[h])
         nc.sync.dma_start(x_list[:], offs)
         for h in range(HALVES):
             nc.sync.dma_start(x_rows[h][:], xf_halves[h])
-        for side, weight in (("g", cb), ("x", ca)):
-            first = WEIGHT_ROW[side]
-            nc.scalar.dma_start(
-                weight_rows[first : first + PACK, :].rearrange("t (b r) -> t b r", r=RUN),
-                weight[0:SLOTS].rearrange("(b t r) o -> t b (r o)", t=PACK, r=RUN),
-            )
-            nc.sync.dma_start(pairs[side][:, 1, :], weight[SLOTS:J].rearrange("(p t) o -> p (t o)", t=PACK))
-        nc.sync.dma_start(row_factor[:], gk.rearrange("(p h) o -> p (h o)", h=HALVES))
+        nc.scalar.dma_start(row_factor[:], gk.rearrange("(p h) o -> p (h o)", h=HALVES))
+        nc.scalar.dma_start(g_pairs[:, :, 1, :], cb.rearrange("(a p t) o -> p a (t o)", a=PASSES, t=PACK))
+        nc.scalar.dma_start(x_pairs[:, :, 1, :], ca.rearrange("(a p t) o -> p a (t o)", a=PASSES, t=PACK))
+        make_identity(nc, identity[:])
+        nc.scalar.activation(out_factor[:], row_factor[:], ACT.Copy, scale=0.02)
 
         banks = {}
 
@@ -68,7 +62,7 @@ def tile_list_moment_sized_sized_sums_kernel(tc, xf, ca, gt, cb, gk, offs, offs2
             offsets = slot_list[:, a * LIST_COLS : (a + 1) * LIST_COLS]
             if on_vector:
                 nc.vector.tensor_copy(
-                    picked[:].bitcast(U32).rearrange("p (t b r) -> p b t r", t=PACK, r=RUN),
+                    picked[:].bitcast(U32).rearrange("p (t s) -> p s t", t=PACK),
                     rows[h][:].bitcast(U32).indirect(offsets),
                 )
                 planes = picked[:].rearrange("p (t s) -> p t s", t=PACK)
@@ -81,9 +75,14 @@ def tile_list_moment_sized_sized_sums_kernel(tc, xf, ca, gt, cb, gk, offs, offs2
             banks[side, h, a] = bank
 
         x_terms = sb.tile([P, PASSES, HALVES + 1, PACK], F32, name="x_terms")
-        zeros = sb.tile([P, PASSES, PACK], F32, name="zeros")
-        nc.vector.memset(zeros[:], 0.0)
-        nc.scalar.activation(x_terms[:, :, HALVES, :], zeros[:], ACT.Copy, bias=0.1)
+        nc.vector.tensor_scalar(
+            x_terms[:, :, HALVES, :],
+            identity[:, 0 : PASSES * PACK].rearrange("p (a t) -> p a t", t=PACK),
+            0.0,
+            0.1,
+            ALU.mult,
+            ALU.add,
+        )
 
         g_turned = {}
         g_top = sb.tile([P, HALVES, PASSES, PACK], F32, name="g_top")
@@ -107,36 +106,28 @@ def tile_list_moment_sized_sized_sums_kernel(tc, xf, ca, gt, cb, gk, offs, offs2
 
         factors = {}
 
-        turned_weights = []
-
-        def turn_weights():
-            bank = ps.tile([P, P], F32, name="turned_weights", tag="bank_g01")
-            nc.tensor.transpose(bank[:], weight_rows[:], identity[:])
-            turned_weights.append(bank)
-
-        def finish_factor(side, a, size):
-            factor = sb.tile([P, PACK], F32, name="factor_%s%d" % (side, a), tag="factor_%s%d" % (side, a), align_bytes=64)
-            if a == 0:
-                inverse = sb.tile([P, PACK], F32, name="inverse_" + side)
-                nc.vector.reciprocal(inverse[:], size[:])
-                weight = turned_weights[0][:, WEIGHT_ROW[side] : WEIGHT_ROW[side] + PACK]
-                nc.vector.tensor_tensor(factor[:], inverse[:], weight, ALU.mult)
-            else:
-                nc.vector.reciprocal(pairs[side][:, 0, :], size[:])
-                nc.vector.tensor_reduce(factor[:], pairs[side][:].rearrange("p i t -> p t i"), AXIS_X, ALU.mult)
-            factors[side, a] = factor[:].unsqueeze(1).to_broadcast([P, P, PACK])
-
         def g_factor(a):
             shifted = sb.tile([P, PACK], F32, name="g_shifted%d" % a, tag="g_shifted%d" % a)
             nc.vector.tensor_scalar(shifted[:], g_top[:, 0, a], 0.2, None, ALU.add)
             size = sb.tile([P, PACK], F32, name="g_size%d" % a)
             nc.vector.scalar_tensor_tensor(size[:], g_top[:, 1, a], 0.2, shifted[:], ALU.add, ALU.max)
-            finish_factor("g", a, size)
+            pair = g_pairs[:, a]
+            nc.vector.reciprocal(pair[:, 0, :], size[:])
+            factor = sb.tile([P, PACK], F32, name="g_factor%d" % a)
+            nc.vector.tensor_reduce(factor[:], pair.rearrange("p i t -> p t i"), AXIS_X, ALU.mult)
+            factors["g", a] = factor[:].unsqueeze(1).to_broadcast([P, P, PACK])
+
+        x_factors = {}
 
         def x_factor(a):
-            size = sb.tile([P, PACK], F32, name="x_size%d" % a)
+            size = sb.tile([P, PACK], F32, name="x_size%d" % a, tag="x_size%d" % a, align_bytes=64)
             nc.vector.tensor_reduce(size[:], x_terms[:, a].rearrange("p i t -> p t i"), AXIS_X, ALU.add)
-            finish_factor("x", a, size)
+            pair = x_pairs[:, a]
+            nc.vector.reciprocal(pair[:, 0, :], size[:])
+            factor = sb.tile([P, PACK], F32, name="x_factor%d" % a)
+            nc.vector.tensor_reduce(factor[:], pair.rearrange("p i t -> p t i"), AXIS_X, ALU.mult)
+            x_factors[a] = factor
+            factors["x", a] = factor[:].unsqueeze(1).to_broadcast([P, P, PACK])
 
         g_rounded = sb.tile([P, PASSES, HALVES, P, PACK], BF16, name="g_rounded", align_bytes=64)
         x_rounded = {}
@@ -150,13 +141,21 @@ def tile_list_moment_sized_sized_sums_kernel(tc, xf, ca, gt, cb, gk, offs, offs2
 
         def x_scale(h, a):
             tile = sb.tile([P, P, PACK], BF16, name="x_rounded%d%d" % (h, a), align_bytes=64)
-            nc.vector.tensor_tensor(tile[:], banks["x", h, a][:].rearrange("p t c -> p c t"), factors["x", a], ALU.mult)
+            if (h, a) == (0, 0):
+                for t in range(PACK):
+                    nc.scalar.activation(
+                        tile[:, :, t], banks["x", h, a][:, t, :], ACT.Copy, scale=x_factors[a][:, t : t + 1]
+                    )
+            else:
+                nc.vector.tensor_tensor(
+                    tile[:], banks["x", h, a][:].rearrange("p t c -> p c t"), factors["x", a], ALU.mult
+                )
             x_rounded[h, a] = tile
 
         operand = {}
 
         def g_quantize():
-            codes = sb.tile([P, PASSES * HALVES * P], U32, name="g_codes", tag="factor_x0", align_bytes=64)
+            codes = sb.tile([P, PASSES * HALVES * P], U32, name="g_codes", tag="x_size1", align_bytes=64)
             scales = sb.tile([P, PASSES * HALVES * P], U8, name="g_scales", align_bytes=64)
             nc.vector.quantize_mx(
                 out=codes[:].bitcast(E5M2), scales=scales[:], in_=g_rounded[:].rearrange("p a h c t -> p (a h c t)")
@@ -180,7 +179,6 @@ def tile_list_moment_sized_sized_sums_kernel(tc, xf, ca, gt, cb, gk, offs, offs2
         gather_and_turn("g", g_rows, g_list, 1, 0, True, "picked_c")
         gather_and_turn("g", g_rows, g_list, 1, 1, False, "picked_a")
         g_stat(0, 1)
-        turn_weights()
         g_stat(1, 0)
         g_factor(0)
         gather_and_turn("x", x_rows, x_list, 0, 0, True, "g_turned00")
@@ -199,16 +197,16 @@ def tile_list_moment_sized_sized_sums_kernel(tc, xf, ca, gt, cb, gk, offs, offs2
             x_scale(h, 0)
         x_factor(1)
         g_quantize()
-        for h in range(HALVES):
-            x_quantize(h, 0)
-        for h in range(HALVES):
-            x_scale(h, 1)
+        x_scale(0, 1)
+        x_quantize(1, 0)
+        x_scale(1, 1)
+        x_quantize(0, 0)
         for h in range(HALVES):
             x_quantize(h, 1)
 
         out_halves = out.rearrange("(p h) q -> h p q", h=HALVES)
         for m in range(HALVES):
-            pair_sums = ps.tile([P, Q, 2], F32, name="pair_sums%d" % m, tag="bank_g%d%d" % (m, m))
+            pair_sums = ps.tile([P, Q, 2], F32, name="pair_sums%d" % m, tag="bank_g%d0" % m)
             for a in range(PASSES):
                 for h in range(HALVES):
                     nc.tensor.matmul_mx(
@@ -223,5 +221,5 @@ def tile_list_moment_sized_sized_sums_kernel(tc, xf, ca, gt, cb, gk, offs, offs2
             set_sums = sb.tile([P, Q], F32, name="set_sums%d" % m)
             nc.vector.tensor_reduce(set_sums[:], pair_sums[:], AXIS_X, ALU.add)
             result = sb.tile([P, Q], F32, name="result%d" % m)
-            nc.vector.tensor_scalar(result[:], set_sums[:], row_factor[:, m : m + 1], 0.02, ALU.mult, ALU.mult)
+            nc.vector.tensor_scalar(result[:], set_sums[:], out_factor[:, m : m + 1], None, ALU.mult)
             nc.sync.dma_start(out_halves[m], result[:])

@@ -23,6 +23,7 @@ SLOTS = P * PACK
 PASSES = J // SLOTS
 HALVES = 2
 LIST_COLS = SLOTS // 16
+STEP = 4
 
 
 def tile_list_moment_sized_sized_sums_kernel(tc, xf, ca, gt, cb, gk, offs, offs2, out):
@@ -115,9 +116,7 @@ def tile_list_moment_sized_sized_sums_kernel(tc, xf, ca, gt, cb, gk, offs, offs2
             nc.vector.reciprocal(pair[:, 0, :], size[:])
             factor = sb.tile([P, PACK], F32, name="g_factor%d" % a)
             nc.vector.tensor_reduce(factor[:], pair.rearrange("p i t -> p t i"), AXIS_X, ALU.mult)
-            factors["g", a] = factor[:].unsqueeze(1).to_broadcast([P, P, PACK])
-
-        x_factors = {}
+            factors["g", a] = factor
 
         def x_factor(a):
             size = sb.tile([P, PACK], F32, name="x_size%d" % a, tag="x_size%d" % a, align_bytes=64)
@@ -126,30 +125,35 @@ def tile_list_moment_sized_sized_sums_kernel(tc, xf, ca, gt, cb, gk, offs, offs2
             nc.vector.reciprocal(pair[:, 0, :], size[:])
             factor = sb.tile([P, PACK], F32, name="x_factor%d" % a)
             nc.vector.tensor_reduce(factor[:], pair.rearrange("p i t -> p t i"), AXIS_X, ALU.mult)
-            x_factors[a] = factor
-            factors["x", a] = factor[:].unsqueeze(1).to_broadcast([P, P, PACK])
+            factors["x", a] = factor
 
         g_rounded = sb.tile([P, PASSES, HALVES, P, PACK], BF16, name="g_rounded", align_bytes=64)
         x_rounded = {}
+
+        def scale_and_weave(engine, woven, planes, factor):
+            engine.tensor_tensor(
+                woven.rearrange("p (c i) t -> p c t i", i=STEP),
+                planes.rearrange("p t (c i) -> p c t i", i=STEP),
+                factor[:].unsqueeze(1).unsqueeze(3).to_broadcast([P, P // STEP, PACK, STEP]),
+                ALU.mult,
+            )
 
         def g_scale(h, a):
             if h == a:
                 engine, source = nc.vector, banks["g", h, a]
             else:
                 engine, source = nc.gpsimd, g_turned[h, a]
-            engine.tensor_tensor(g_rounded[:, a, h], source[:].rearrange("p t c -> p c t"), factors["g", a], ALU.mult)
+            scale_and_weave(engine, g_rounded[:, a, h], source[:], factors["g", a])
 
         def x_scale(h, a):
             tile = sb.tile([P, P, PACK], BF16, name="x_rounded%d%d" % (h, a), align_bytes=64)
             if (h, a) == (0, 0):
                 for t in range(PACK):
                     nc.scalar.activation(
-                        tile[:, :, t], banks["x", h, a][:, t, :], ACT.Copy, scale=x_factors[a][:, t : t + 1]
+                        tile[:, :, t], banks["x", h, a][:, t, :], ACT.Copy, scale=factors["x", a][:, t : t + 1]
                     )
             else:
-                nc.vector.tensor_tensor(
-                    tile[:], banks["x", h, a][:].rearrange("p t c -> p c t"), factors["x", a], ALU.mult
-                )
+                scale_and_weave(nc.vector, tile[:], banks["x", h, a][:], factors["x", a])
             x_rounded[h, a] = tile
 
         operand = {}

from contextlib import ExitStack

import concourse.mybir as mybir
from concourse.masks import make_identity

K, J, N, T, Q = 256, 1024, 256, 2048, 64
FLOPS = 2 * K * J * N

F32 = mybir.dt.float32
BF16 = mybir.dt.bfloat16
U32 = mybir.dt.uint32
U16 = mybir.dt.uint16
U8 = mybir.dt.uint8
E4M3 = mybir.dt.float8_e4m3fn_x4
E5M2 = mybir.dt.float8_e5m2_x4
ALU = mybir.AluOpType
ACT = mybir.ActivationFunctionType
AXIS_X = mybir.AxisListType.X

P = 128
PACK = 4
SLOTS = P * PACK
PASSES = J // SLOTS
HALVES = 2
LIST_COLS = SLOTS // 16
STEP = 4


def tile_list_moment_sized_sized_sums_kernel(tc, xf, ca, gt, cb, gk, offs, offs2, out):
    nc = tc.nc
    with ExitStack() as ctx:
        sb = ctx.enter_context(tc.tile_pool(name="sb", bufs=1))
        ps = ctx.enter_context(tc.psum_pool(name="ps", bufs=1))

        g_list = sb.tile([P, J // 16], U16, name="g_list")
        x_list = sb.tile([P, J // 16], U16, name="x_list")
        g_rows = [sb.tile([P, T], F32, name="g_rows%d" % h) for h in range(HALVES)]
        x_rows = [sb.tile([P, T], F32, name="x_rows%d" % h) for h in range(HALVES)]
        g_pairs = sb.tile([P, PASSES, 2, PACK], F32, name="g_pairs")
        x_pairs = sb.tile([P, PASSES, 2, PACK], F32, name="x_pairs")
        row_factor = sb.tile([P, HALVES], F32, name="row_factor")
        out_factor = sb.tile([P, HALVES], F32, name="out_factor")
        identity = sb.tile([P, P], F32, name="identity")

        gt_halves = gt.rearrange("(p h) v -> h p v", h=HALVES)
        xf_halves = xf.rearrange("(p h) v -> h p v", h=HALVES)
        nc.sync.dma_start(g_list[:], offs2)
        for h in range(HALVES):
            nc.sync.dma_start(g_rows[h][:], gt_halves[h])
        nc.sync.dma_start(x_list[:], offs)
        for h in range(HALVES):
            nc.sync.dma_start(x_rows[h][:], xf_halves[h])
        nc.scalar.dma_start(row_factor[:], gk.rearrange("(p h) o -> p (h o)", h=HALVES))
        nc.scalar.dma_start(g_pairs[:, :, 1, :], cb.rearrange("(a p t) o -> p a (t o)", a=PASSES, t=PACK))
        nc.scalar.dma_start(x_pairs[:, :, 1, :], ca.rearrange("(a p t) o -> p a (t o)", a=PASSES, t=PACK))
        make_identity(nc, identity[:])
        nc.scalar.activation(out_factor[:], row_factor[:], ACT.Copy, scale=0.02)

        banks = {}

        def gather_and_turn(side, rows, slot_list, h, a, on_vector, buffer):
            picked = sb.tile([P, SLOTS], F32, name="picked_%s%d%d" % (side, h, a), tag=buffer)
            offsets = slot_list[:, a * LIST_COLS : (a + 1) * LIST_COLS]
            if on_vector:
                nc.vector.tensor_copy(
                    picked[:].bitcast(U32).rearrange("p (t s) -> p s t", t=PACK),
                    rows[h][:].bitcast(U32).indirect(offsets),
                )
                planes = picked[:].rearrange("p (t s) -> p t s", t=PACK)
            else:
                nc.scalar.activation(picked[:], rows[h][:].indirect(offsets), ACT.Copy)
                planes = picked[:].rearrange("p (s t) -> p t s", t=PACK)
            bank = ps.tile([P, PACK, P], F32, name="turned_%s%d%d" % (side, h, a), tag="bank_%s%d%d" % (side, h, a))
            for t in range(PACK):
                nc.tensor.transpose(bank[:, t, :], planes[:, t, :], identity[:])
            banks[side, h, a] = bank

        x_terms = sb.tile([P, PASSES, HALVES + 1, PACK], F32, name="x_terms")
        nc.vector.tensor_scalar(
            x_terms[:, :, HALVES, :],
            identity[:, 0 : PASSES * PACK].rearrange("p (a t) -> p a t", t=PACK),
            0.0,
            0.1,
            ALU.mult,
            ALU.add,
        )

        g_turned = {}
        g_top = sb.tile([P, HALVES, PASSES, PACK], F32, name="g_top")

        def g_stat(h, a):
            tile = sb.tile([P, PACK, P], F32, name="g_turned%d%d" % (h, a), tag="g_turned%d%d" % (h, a))
            nc.scalar.copy(tile[:], banks["g", h, a][:])
            nc.vector.tensor_reduce(g_top[:, h, a, :], tile[:], AXIS_X, ALU.max, apply_absolute_value=True)
            g_turned[h, a] = tile

        def x_stat(h, a):
            unused = sb.tile([P, PACK, P], BF16, name="x_magnitude%d%d" % (h, a))
            for t in range(PACK):
                nc.scalar.activation(
                    unused[:, t, :],
                    banks["x", h, a][:, t, :],
                    ACT.Abs,
                    scale=1.0 / K,
                    accum_out=x_terms[:, a, h, t : t + 1],
                )

        factors = {}

        def g_factor(a):
            shifted = sb.tile([P, PACK], F32, name="g_shifted%d" % a, tag="g_shifted%d" % a)
            nc.vector.tensor_scalar(shifted[:], g_top[:, 0, a], 0.2, None, ALU.add)
            size = sb.tile([P, PACK], F32, name="g_size%d" % a)
            nc.vector.scalar_tensor_tensor(size[:], g_top[:, 1, a], 0.2, shifted[:], ALU.add, ALU.max)
            pair = g_pairs[:, a]
            nc.vector.reciprocal(pair[:, 0, :], size[:])
            factor = sb.tile([P, PACK], F32, name="g_factor%d" % a)
            nc.vector.tensor_reduce(factor[:], pair.rearrange("p i t -> p t i"), AXIS_X, ALU.mult)
            factors["g", a] = factor

        def x_factor(a):
            size = sb.tile([P, PACK], F32, name="x_size%d" % a, tag="x_size%d" % a, align_bytes=64)
            nc.vector.tensor_reduce(size[:], x_terms[:, a].rearrange("p i t -> p t i"), AXIS_X, ALU.add)
            pair = x_pairs[:, a]
            nc.vector.reciprocal(pair[:, 0, :], size[:])
            factor = sb.tile([P, PACK], F32, name="x_factor%d" % a)
            nc.vector.tensor_reduce(factor[:], pair.rearrange("p i t -> p t i"), AXIS_X, ALU.mult)
            factors["x", a] = factor

        g_rounded = sb.tile([P, PASSES, HALVES, P, PACK], BF16, name="g_rounded", align_bytes=64)
        x_rounded = {}

        def scale_and_weave(engine, woven, planes, factor):
            engine.tensor_tensor(
                woven.rearrange("p (c i) t -> p c t i", i=STEP),
                planes.rearrange("p t (c i) -> p c t i", i=STEP),
                factor[:].unsqueeze(1).unsqueeze(3).to_broadcast([P, P // STEP, PACK, STEP]),
                ALU.mult,
            )

        def g_scale(h, a):
            if h == a:
                engine, source = nc.vector, banks["g", h, a]
            else:
                engine, source = nc.gpsimd, g_turned[h, a]
            scale_and_weave(engine, g_rounded[:, a, h], source[:], factors["g", a])

        def x_scale(h, a):
            tile = sb.tile([P, P, PACK], BF16, name="x_rounded%d%d" % (h, a), align_bytes=64)
            if (h, a) == (0, 0):
                for t in range(PACK):
                    nc.scalar.activation(
                        tile[:, :, t], banks["x", h, a][:, t, :], ACT.Copy, scale=factors["x", a][:, t : t + 1]
                    )
            else:
                scale_and_weave(nc.vector, tile[:], banks["x", h, a][:], factors["x", a])
            x_rounded[h, a] = tile

        operand = {}

        def g_quantize():
            codes = sb.tile([P, PASSES * HALVES * P], U32, name="g_codes", tag="x_size1", align_bytes=64)
            scales = sb.tile([P, PASSES * HALVES * P], U8, name="g_scales", align_bytes=64)
            nc.vector.quantize_mx(
                out=codes[:].bitcast(E5M2), scales=scales[:], in_=g_rounded[:].rearrange("p a h c t -> p (a h c t)")
            )
            for a in range(PASSES):
                for h in range(HALVES):
                    cols = slice((a * HALVES + h) * P, (a * HALVES + h + 1) * P)
                    operand["g", h, a] = (codes[:, cols].bitcast(E5M2), scales[:, cols])

        def x_quantize(h, a):
            codes = sb.tile([P, P], U32, name="x_codes%d%d" % (h, a), align_bytes=64)
            scales = sb.tile([P, P], U8, name="x_scales%d%d" % (h, a), align_bytes=64)
            nc.vector.quantize_mx(
                out=codes[:].bitcast(E4M3), scales=scales[:], in_=x_rounded[h, a][:].rearrange("p c t -> p (c t)")
            )
            operand["x", h, a] = (codes[:].bitcast(E4M3), scales[:])

        gather_and_turn("g", g_rows, g_list, 0, 0, True, "picked_a")
        gather_and_turn("g", g_rows, g_list, 0, 1, False, "picked_b")
        g_stat(0, 0)
        gather_and_turn("g", g_rows, g_list, 1, 0, True, "picked_c")
        gather_and_turn("g", g_rows, g_list, 1, 1, False, "picked_a")
        g_stat(0, 1)
        g_stat(1, 0)
        g_factor(0)
        gather_and_turn("x", x_rows, x_list, 0, 0, True, "g_turned00")
        gather_and_turn("x", x_rows, x_list, 0, 1, False, "picked_c")
        gather_and_turn("x", x_rows, x_list, 1, 0, True, "g_shifted0")
        g_stat(1, 1)
        g_factor(1)
        gather_and_turn("x", x_rows, x_list, 1, 1, False, "picked_a")
        for a in range(PASSES):
            for h in range(HALVES):
                x_stat(h, a)
        for h, a in ((1, 0), (0, 0), (0, 1), (1, 1)):
            g_scale(h, a)
        x_factor(0)
        for h in range(HALVES):
            x_scale(h, 0)
        x_factor(1)
        g_quantize()
        x_scale(0, 1)
        x_quantize(1, 0)
        x_scale(1, 1)
        x_quantize(0, 0)
        for h in range(HALVES):
            x_quantize(h, 1)

        out_halves = out.rearrange("(p h) q -> h p q", h=HALVES)
        for m in range(HALVES):
            pair_sums = ps.tile([P, Q, 2], F32, name="pair_sums%d" % m, tag="bank_g%d0" % m)
            for a in range(PASSES):
                for h in range(HALVES):
                    nc.tensor.matmul_mx(
                        out=pair_sums[:].rearrange("p q e -> p (q e)"),
                        lhsT=operand["x", m, a][0],
                        lhsT_scale=operand["x", m, a][1],
                        rhs=operand["g", h, a][0],
                        rhs_scale=operand["g", h, a][1],
                        start=(a == 0 and h == 0),
                        stop=(a == PASSES - 1 and h == HALVES - 1),
                    )
            set_sums = sb.tile([P, Q], F32, name="set_sums%d" % m)
            nc.vector.tensor_reduce(set_sums[:], pair_sums[:], AXIS_X, ALU.add)
            result = sb.tile([P, Q], F32, name="result%d" % m)
            nc.vector.tensor_scalar(result[:], set_sums[:], out_factor[:, m : m + 1], None, ALU.mult)
            nc.sync.dma_start(out_halves[m], result[:])
